import numpy as np
import ml_dtypes


def mxq(x, axis, fmt="e4m3"):
    dtype, down = {"e4m3": (ml_dtypes.float8_e4m3fn, 7), "e5m2": (ml_dtypes.float8_e5m2, 14)}[fmt]
    v = np.moveaxis(np.asarray(x, np.float32).astype(ml_dtypes.bfloat16).astype(np.float64), axis, -1)
    blocks = v.reshape(v.shape[:-1] + (-1, 32))
    amax = np.abs(blocks).max(-1, keepdims=True)
    byte = np.maximum(np.where(amax > 0, np.frexp(amax)[1] - 1 + 127, 0) - down, 1)
    scale = np.exp2(byte - 127.0)
    codes = (blocks / scale).astype(np.float32).astype(dtype).astype(np.float64)
    return np.moveaxis((codes * scale).reshape(v.shape), -1, axis)


WIDE = False


def mx_kscale(k):
    if not WIDE:
        return np.ones(k)
    levels = np.array([10, -10, 5, -5, 0])
    if k % 512:
        return np.exp2(np.random.permutation(np.resize(levels, k // 32))).repeat(32)
    a = np.empty((k // 512, 16))
    for p in range(k // 512):
        a[p, :8] = np.random.permutation(np.resize(levels, 8))
        for g in range(8):
            far = levels[np.abs(levels - a[p, g]) >= 10]
            a[p, g + 8] = far[np.random.randint(len(far))]
    return np.exp2(a.ravel()).repeat(32)


def f64(x):
    return np.asarray(x).astype(np.float64)


def striped(idx):
    return np.tile(idx.reshape(-1, 16).T, (8, 1)).astype(np.uint16)


def unstriped(offs):
    return offs[:16].T.reshape(-1).astype(np.int64)


E2M1 = np.array([0.0, 0.5, 1.0, 1.5, 2.0, 3.0, 4.0, 6.0, -0.0, -0.5, -1.0, -1.5, -2.0, -3.0, -4.0, -6.0])


def pack_weight(w, fmt):
    k, n = w.shape
    w = f64(np.asarray(w, np.float32).astype(ml_dtypes.bfloat16)).reshape(k // 32, 32, n)
    amax = np.abs(w).max(1)
    if fmt == "e4m3":
        byte = np.frexp(amax)[1] - 1 + 127 - 7
    else:
        mant, ex = np.frexp(amax / 6.0)
        byte = np.where(mant > 0.5, ex, ex - 1) + 127
    byte = np.clip(np.where(amax > 0, byte, 1), 1, 254)
    scaled = (w * np.exp2(127.0 - byte)[:, None, :]).reshape(k, n).astype(np.float32)
    by_word = np.ascontiguousarray(scaled.reshape(k // 512, 128, 4, n).transpose(0, 1, 3, 2))
    if fmt == "e4m3":
        words = by_word.astype(ml_dtypes.float8_e4m3fn).view(np.uint8)
    else:
        c = by_word.astype(ml_dtypes.float4_e2m1fn).view(np.uint8) & 0xF
        words = (c[..., 0::2] | (c[..., 1::2] << 4)).reshape(k // 512, 128, 2 * n)
    return np.ascontiguousarray(words), np.ascontiguousarray(byte.astype(np.uint8).reshape(k // 512, 16, n))


def unpack_weight(words, scales, fmt):
    g, _, n = scales.shape
    words = np.ascontiguousarray(words).reshape(g, 128, n, -1)
    if fmt == "e4m3":
        vals = words.view(ml_dtypes.float8_e4m3fn).astype(np.float64)
    else:
        nib = np.empty((g, 128, n, 4), np.uint8)
        nib[..., 0::2] = words & 0xF
        nib[..., 1::2] = words >> 4
        vals = E2M1[nib]
    vals = vals * np.repeat(np.exp2(scales.astype(np.float64) - 127.0), 8, axis=1)[..., None]
    return vals.transpose(0, 1, 3, 2).reshape(g * 512, n)


def gelu(v):
    return 0.5 * v * (1.0 + np.tanh(np.sqrt(2.0 / np.pi) * (v + 0.044715 * v**3)))


K, H, T, S, S2, T3, P = 512, 1024, 4096, 1024, 512, 2048, 512


def setup_inputs():
    n = np.random.standard_normal
    s = mx_kscale(K)[:, None]
    u = mx_kscale(H)[:, None]
    d = {}
    d["tab_words"], d["tab_scales"] = pack_weight(n((K, T)) * s, "e4m3")
    d["offs"] = striped(np.random.permutation(T)[:S])
    d["tab2_words"], d["tab2_scales"] = pack_weight(n((H, T3)) / H ** 0.5 / u, "e4m3")
    d["offs2"] = striped(np.random.permutation(T3)[:S2])
    d["pos1"] = striped(np.random.permutation(S)[:P])
    d["pos2"] = striped(np.random.permutation(S)[:P])
    d["w1"] = (1.2 * n((K, H)) / K ** 0.5 / s).astype(np.float32)
    d["w4_words"], d["w4_scales"] = pack_weight(1.2 * n((K, H)) / K ** 0.5 / s, "e2m1")
    d["rest"] = (0.6 * n(H)).astype(np.float32)
    d["gain"] = (np.exp(0.3 * n(H)) * u[:, 0]).astype(np.float32)
    d["shot"] = np.exp(0.4 * n((S2, P))).astype(np.float32)
    return d


def reference(tab_words, tab_scales, offs, tab2_words, tab2_scales, offs2, pos1, pos2,
              w1, w4_words, w4_scales, rest, gain, shot):
    v = unpack_weight(tab_words, tab_scales, "e4m3")[:, unstriped(offs)]
    v2 = unpack_weight(tab2_words, tab2_scales, "e4m3")[:, unstriped(offs2)]
    w4 = unpack_weight(w4_words, w4_scales, "e2m1")
    shape = mxq(f64(w1), 0, "e4m3").T @ v
    stress = w4.T @ v
    h = np.tanh(shape * stress + f64(rest)[:, None]) * f64(gain)[:, None]
    e = v2.T @ mxq(h, 0, "e4m3")
    incoming = e[:, unstriped(pos1)]
    outgoing = e[:, unstriped(pos2)]
    return f64(shot) * incoming - outgoing

@@ -1,0 +1,232 @@
+from contextlib import ExitStack
+
+import concourse.mybir as mybir
+
+K, H, T, S, S2, T3, NP = 512, 1024, 4096, 1024, 512, 2048, 512
+FLOPS = 2 * K * H * S * 2 + 2 * H * S2 * S
+
+F32 = mybir.dt.float32
+BF16 = mybir.dt.bfloat16
+I32 = mybir.dt.int32
+U32 = mybir.dt.uint32
+U16 = mybir.dt.uint16
+U8 = mybir.dt.uint8
+FP8X4 = mybir.dt.float8_e4m3fn_x4
+FP4X4 = mybir.dt.float4_e2m1fn_x4
+ACT = mybir.ActivationFunctionType
+ALU = mybir.AluOpType
+
+P = 128
+PACK = 4
+PASS = P * PACK
+HALF = 512
+
+
+def tile_list_mouth_piece_chooser_kernel(tc, tab_words, tab_scales, offs, tab2_words, tab2_scales, offs2,
+                                                  pos1, pos2, w1, w4_words, w4_scales, rest, gain, shot, out):
+    nc = tc.nc
+    with ExitStack() as ctx:
+        keep = ctx.enter_context(tc.tile_pool(name="keep", bufs=1))
+        work = ctx.enter_context(tc.tile_pool(name="work", bufs=2))
+        psum = ctx.enter_context(tc.psum_pool(name="psum", bufs=1))
+
+        offs_t = keep.tile([P, S // 16], U16, name="offs_t")
+        offs2_t = keep.tile([P, S2 // 16], U16, name="offs2_t")
+        pos1_t = keep.tile([P, NP // 16], U16, name="pos1_t")
+        pos2_t = keep.tile([P, NP // 16], U16, name="pos2_t")
+
+        w4s_raw = keep.tile([P, H], U8, name="w4s_raw", tag="scale_rows", align_bytes=64)
+        tab_s = keep.tile([P, T], U8, name="tab_s", align_bytes=64)
+        warm = keep.tile([P, 2], F32, name="warm")
+        nc.gpsimd.memset(w4s_raw[:].bitcast(I32), 0)
+        nc.vector.memset(tab_s[:].bitcast(I32), 0)
+        nc.vector.memset(warm[:, 0:1], 0.0)
+
+        w1_rows = w1.rearrange("(p j) c -> p j c", j=PACK)
+
+        def load_w1(b):
+            raw = keep.tile([P, PACK, PASS], F32, name="w1_raw", tag="stage")
+            nc.sync.dma_start(raw[:], w1_rows[:, :, b * PASS:(b + 1) * PASS])
+            return raw
+
+        nc.sync.dma_start(offs_t[:], offs)
+        w4w_raw = keep.tile([P, 2 * H], U8, name="w4w_raw", align_bytes=64)
+        nc.sync.dma_start(w4w_raw[:].bitcast(I32), w4_words[0].bitcast(I32))
+        nc.sync.dma_start(offs2_t[:], offs2)
+        for q in range(4):
+            nc.scalar.dma_start(tab_s[32 * q:32 * q + 4, :].bitcast(I32), tab_scales[0, 4 * q:4 * q + 4, :].bitcast(I32))
+        w1_raw0 = load_w1(0)
+        tab_w = keep.tile([P, T], I32, name="tab_w", tag="table", align_bytes=64)
+        nc.sync.dma_start(tab_w[:], tab_words[0].rearrange("p n t -> p (n t)").bitcast(I32))
+        nc.sync.dma_start(pos1_t[:], pos1)
+        nc.sync.dma_start(pos2_t[:], pos2)
+
+        for q in range(4):
+            nc.gpsimd.dma_start(w4s_raw[32 * q:32 * q + 4, :].bitcast(I32), w4_scales[0, 4 * q:4 * q + 4, :].bitcast(I32))
+        rest_t = keep.tile([P, 2, PACK], F32, name="rest_t")
+        gain_t = keep.tile([P, 2, PACK], F32, name="gain_t")
+        nc.gpsimd.dma_start(rest_t[:], rest.rearrange("(b p t) -> p b t", b=2, t=PACK))
+        nc.gpsimd.dma_start(gain_t[:], gain.rearrange("(b p t) -> p b t", b=2, t=PACK))
+
+        nc.scalar.activation(out=warm[:, 1:2], in_=warm[:, 0:1], func=ACT.Tanh)
+
+        w4w, w4s, w1w, w1s = [], [], [], []
+
+        def deal_w4(b):
+            words = keep.tile([P, 2 * PASS], U8, name=f"w4w{b}", align_bytes=64)
+            scales = keep.tile([P, PASS], U8, name=f"w4s{b}", align_bytes=64)
+            nc.vector.tensor_copy(
+                out=words[:].bitcast(U16).rearrange("p (t c i) -> p c t i", t=PACK, i=8),
+                in_=w4w_raw[:, 2 * PASS * b:2 * PASS * (b + 1)].bitcast(U16).rearrange("p (c i t) -> p c t i", t=PACK, i=8))
+            nc.vector.tensor_copy(
+                out=scales[:].rearrange("p (t c i) -> p c t i", t=PACK, i=16),
+                in_=w4s_raw[:, PASS * b:PASS * (b + 1)].rearrange("p (c i t) -> p c t i", t=PACK, i=16))
+            w4w.append(words)
+            w4s.append(scales)
+
+        def round_w1(raw, grouped, lo, hi):
+            nc.scalar.copy(out=grouped[:].rearrange("p (t m j) -> p m t j", t=PACK, j=PACK)[:, lo:hi],
+                           in_=raw[:].rearrange("p j (m t) -> p m t j", t=PACK)[:, lo:hi])
+
+        def quantise_w1(b, grouped):
+            words = keep.tile([P, PASS], U32, name=f"w1w{b}", align_bytes=64)
+            scales = keep.tile([P, PASS], U8, name=f"w1s{b}", align_bytes=64)
+            nc.vector.quantize_mx(out=words[:].bitcast(FP8X4), scales=scales[:], in_=grouped[:])
+            w1w.append(words)
+            w1s.append(scales)
+
+        vs, vw = [], []
+
+        def gather_v_scales(h):
+            t = keep.tile([P, HALF], U8, name=f"vs{h}", align_bytes=64)
+            nc.vector.tensor_copy(t[:], tab_s[:].indirect(offs_t[:, 32 * h:32 * (h + 1)]))
+            vs.append(t)
+
+        def gather_v_words(h):
+            t = keep.tile([P, HALF], U32, name=f"vw{h}", align_bytes=64)
+            nc.vector.tensor_copy(t[:], tab_w[:].bitcast(U32).indirect(offs_t[:, 32 * h:32 * (h + 1)]))
+            vw.append(t)
+
+        w1_bf0 = keep.tile([P, PACK * PASS], BF16, name="w1_bf0", align_bytes=64)
+        w1_bf1 = keep.tile([P, PACK * PASS], BF16, name="w1_bf1", align_bytes=64)
+        round_w1(w1_raw0, w1_bf0, 0, P)
+        gather_v_scales(0)
+        gather_v_scales(1)
+        deal_w4(0)
+        deal_w4(1)
+        quantise_w1(0, w1_bf0)
+        gather_v_words(0)
+        gather_v_words(1)
+
+        w1_raw1 = load_w1(1)
+        tab2_s = keep.tile([P, T3], U8, name="tab2_s", tag="scale_rows", align_bytes=64)
+        nc.vector.memset(tab2_s[:].bitcast(I32), 0)
+        for q in range(4):
+            nc.sync.dma_start(tab2_s[32 * q:32 * q + 8, :].bitcast(I32), tab2_scales[:, 4 * q:4 * q + 4, :].bitcast(I32))
+        v2s = keep.tile([P, S2], U8, name="v2s", align_bytes=64)
+        tab2_w = keep.tile([P, 2 * T3], I32, name="tab2_w", tag="table", align_bytes=64)
+        for a in range(2):
+            nc.sync.dma_start(tab2_w[:, a * T3:(a + 1) * T3], tab2_words[a].rearrange("p n t -> p (n t)").bitcast(I32))
+
+        v2w = []
+
+        def gather_v2_words(a):
+            t = keep.tile([P, S2], U32, name=f"v2w{a}", align_bytes=64)
+            nc.vector.tensor_copy(t[:], tab2_w[:, a * T3:(a + 1) * T3].bitcast(U32).indirect(offs2_t[:]))
+            v2w.append(t)
+
+        neg_e = [keep.tile([P, S], F32, name=f"neg_e{m}") for m in range(4)]
+
+        groups = [(0, 0, 512), (0, 512, 512), (1, 0, 512), (1, 512, 256), (1, 768, 256)]
+        bounded, hw, hs = {}, {}, {}
+
+        def unit(g, t):
+            b, c0, width = groups[g]
+            h, lo = divmod(c0, HALF)
+            cols = slice(lo, lo + width)
+            if t == 0:
+                bounded[g] = work.tile([P, PACK, width], F32, name="bounded", tag="bounded")
+            stress_ps = psum.tile([P, width], F32, name="stress_ps", tag="stress_ps", bufs=3)
+            nc.tensor.matmul_mx(out=stress_ps[:], lhsT=w4w[b][:, 2 * P * t:2 * P * (t + 1)].bitcast(FP4X4),
+                                lhsT_scale=w4s[b][:, P * t:P * (t + 1)], rhs=vw[h][:, cols].bitcast(FP8X4),
+                                rhs_scale=vs[h][:, cols], start=True, stop=True)
+            shape_ps = psum.tile([P, width], F32, name="shape_ps", tag="shape_ps", bufs=3)
+            nc.tensor.matmul_mx(out=shape_ps[:], lhsT=w1w[b][:, P * t:P * (t + 1)].bitcast(FP8X4),
+                                lhsT_scale=w1s[b][:, P * t:P * (t + 1)], rhs=vw[h][:, cols].bitcast(FP8X4),
+                                rhs_scale=vs[h][:, cols], start=True, stop=True)
+            stress = work.tile([P, width], F32, name="stress", tag="stress", bufs=4)
+            nc.scalar.copy(out=stress[:], in_=stress_ps[:])
+            prod = work.tile([P, width], F32, name="prod", tag="prod", bufs=3)
+            nc.vector.tensor_tensor(out=prod[:], in0=shape_ps[:], in1=stress[:], op=ALU.mult)
+            nc.scalar.activation(out=bounded[g][:, t, :], in_=prod[:], func=ACT.Tanh, bias=rest_t[:, b, t:t + 1])
+
+        h_bf = {}
+
+        def apply_gain(g):
+            b, c0, width = groups[g]
+            h_bf[g] = work.tile([P, PACK * width], BF16, name="h_bf", tag="h_bf", align_bytes=64)
+            nc.vector.tensor_tensor(
+                out=h_bf[g][:].rearrange("p (c i t) -> p c t i", t=PACK, i=4),
+                in0=bounded[g][:].rearrange("p t (c i) -> p c t i", i=4),
+                in1=gain_t[:, b, :].unsqueeze(1).unsqueeze(3).to_broadcast([P, width // 4, PACK, 4]),
+                op=ALU.mult)
+
+        def quantise_h(g):
+            b, c0, width = groups[g]
+            hw[g] = keep.tile([P, width], U32, name=f"hw{g}", align_bytes=64)
+            hs[g] = keep.tile([P, width], U8, name=f"hs{g}", align_bytes=64)
+            nc.vector.quantize_mx(out=hw[g][:].bitcast(FP8X4), scales=hs[g][:], in_=h_bf[g][:])
+
+        def scores(g):
+            b, c0, width = groups[g]
+            g0, lo = divmod(c0, HALF)
+            for m in range(4):
+                e_ps = psum.tile([P, width], F32, name="e_ps", tag="e_ps", bufs=2)
+                for a, (gg, cols) in enumerate(((g0, slice(lo, lo + width)), (g, slice(0, width)))):
+                    nc.tensor.matmul_mx(out=e_ps[:], lhsT=v2w[a][:, P * m:P * (m + 1)].bitcast(FP8X4),
+                                        lhsT_scale=v2s[4 * a:P, P * m:P * (m + 1)], rhs=hw[gg][:, cols].bitcast(FP8X4),
+                                        rhs_scale=hs[gg][:, cols], start=(a == 0), stop=(a == 1))
+                nc.scalar.activation(out=neg_e[m][:, c0:c0 + width], in_=e_ps[:], func=ACT.Copy, scale=-1.0)
+
+        shot_t = keep.tile([P, 4, NP], F32, name="shot_t", tag="stage")
+        for g in range(len(groups)):
+            for t in range(PACK):
+                unit(g, t)
+                u = PACK * g + t
+                if g > 0 and t == 1:
+                    apply_gain(g - 1)
+                if g > 0 and t == 2:
+                    quantise_h(g - 1)
+                if g > 2 and t == 3:
+                    scores(g - 1)
+                if 2 <= u < 6:
+                    round_w1(w1_raw1, w1_bf1, 32 * (u - 2), 32 * (u - 1))
+                if u == 5:
+                    nc.sync.dma_start(shot_t[:], shot.rearrange("(m p) n -> p m n", p=P))
+                if u == 6:
+                    quantise_w1(1, w1_bf1)
+                if u == 8:
+                    nc.vector.tensor_copy(v2s[:], tab2_s[:].indirect(offs2_t[:]))
+                if u in (10, 11):
+                    gather_v2_words(u - 10)
+        last = len(groups) - 1
+        apply_gain(last)
+        quantise_h(last)
+        scores(last)
+
+        scaled = {}
+
+        def incoming(m):
+            scaled[m] = work.tile([P, NP], F32, name="scaled", tag="scaled")
+            nc.vector.tensor_tensor(scaled[m][:], neg_e[m][:].indirect(pos1_t[:]), shot_t[:, m, :], ALU.mult)
+
+        def outgoing(m):
+            res = work.tile([P, NP], F32, name="res", tag="res", bufs=4)
+            nc.vector.tensor_tensor(res[:], neg_e[m][:].indirect(pos2_t[:]), scaled[m][:], ALU.subtract)
+            nc.sync.dma_start(out[P * m:P * (m + 1), :], res[:])
+
+        incoming(0)
+        for m in range(4):
+            if m < 3:
+                incoming(m + 1)
+            outgoing(m)

@@ -37,7 +37,7 @@ def tile_list_mouth_piece_chooser_kernel(tc, tab_words, tab_scales, offs, tab2_w
 
         w4s_raw = keep.tile([P, H], U8, name="w4s_raw", tag="scale_rows", align_bytes=64)
         tab_s = keep.tile([P, T], U8, name="tab_s", align_bytes=64)
-        warm = keep.tile([P, 2], F32, name="warm")
+        warm = keep.tile([P, 2], F32, name="warm", tag="rows")
         nc.gpsimd.memset(w4s_raw[:].bitcast(I32), 0)
         nc.vector.memset(tab_s[:].bitcast(I32), 0)
         nc.vector.memset(warm[:, 0:1], 0.0)
@@ -49,43 +49,42 @@ def tile_list_mouth_piece_chooser_kernel(tc, tab_words, tab_scales, offs, tab2_w
             nc.sync.dma_start(raw[:], w1_rows[:, :, b * PASS:(b + 1) * PASS])
             return raw
 
-        nc.sync.dma_start(offs_t[:], offs)
-        w4w_raw = keep.tile([P, 2 * H], U8, name="w4w_raw", align_bytes=64)
+        w4w_raw = keep.tile([P, 2 * H], U8, name="w4w_raw", tag="table", align_bytes=64)
         nc.sync.dma_start(w4w_raw[:].bitcast(I32), w4_words[0].bitcast(I32))
+        nc.sync.dma_start(offs_t[:], offs)
         nc.sync.dma_start(offs2_t[:], offs2)
         for q in range(4):
             nc.scalar.dma_start(tab_s[32 * q:32 * q + 4, :].bitcast(I32), tab_scales[0, 4 * q:4 * q + 4, :].bitcast(I32))
-        w1_raw0 = load_w1(0)
-        tab_w = keep.tile([P, T], I32, name="tab_w", tag="table", align_bytes=64)
-        nc.sync.dma_start(tab_w[:], tab_words[0].rearrange("p n t -> p (n t)").bitcast(I32))
         nc.sync.dma_start(pos1_t[:], pos1)
         nc.sync.dma_start(pos2_t[:], pos2)
+        w1_raw0 = load_w1(0)
+        w4w = keep.tile([P, 2 * H], U8, name="w4w", align_bytes=64)
+        nc.vector.tensor_copy(
+            out=w4w[:].bitcast(U16).rearrange("p (b t c i) -> p b c t i", b=2, t=PACK, i=8),
+            in_=w4w_raw[:].bitcast(U16).rearrange("p (b c i t) -> p b c t i", b=2, t=PACK, i=8))
+        tab_w = keep.tile([P, T], I32, name="tab_w", tag="table", align_bytes=64)
+        nc.sync.dma_start(tab_w[:], tab_words[0].rearrange("p n t -> p (n t)").bitcast(I32))
 
         for q in range(4):
-            nc.gpsimd.dma_start(w4s_raw[32 * q:32 * q + 4, :].bitcast(I32), w4_scales[0, 4 * q:4 * q + 4, :].bitcast(I32))
-        rest_t = keep.tile([P, 2, PACK], F32, name="rest_t")
-        gain_t = keep.tile([P, 2, PACK], F32, name="gain_t")
-        nc.gpsimd.dma_start(rest_t[:], rest.rearrange("(b p t) -> p b t", b=2, t=PACK))
-        nc.gpsimd.dma_start(gain_t[:], gain.rearrange("(b p t) -> p b t", b=2, t=PACK))
-
+            queue = nc.scalar if q < 3 else nc.gpsimd
+            queue.dma_start(w4s_raw[32 * q:32 * q + 4, :].bitcast(I32), w4_scales[0, 4 * q:4 * q + 4, :].bitcast(I32))
         nc.scalar.activation(out=warm[:, 1:2], in_=warm[:, 0:1], func=ACT.Tanh)
+        rows = keep.tile([P, 2, 2, PACK], F32, name="rows", tag="rows")
+        rest_t, gain_t = rows[:, 0], rows[:, 1]
+        nc.gpsimd.dma_start(rest_t, rest.rearrange("(b p t) -> p b t", b=2, t=PACK))
+        nc.gpsimd.dma_start(gain_t, gain.rearrange("(b p t) -> p b t", b=2, t=PACK))
 
-        w4w, w4s, w1w, w1s = [], [], [], []
+        w4s, w1w, w1s = [], [], []
 
         def deal_w4(b):
-            words = keep.tile([P, 2 * PASS], U8, name=f"w4w{b}", align_bytes=64)
             scales = keep.tile([P, PASS], U8, name=f"w4s{b}", align_bytes=64)
-            nc.vector.tensor_copy(
-                out=words[:].bitcast(U16).rearrange("p (t c i) -> p c t i", t=PACK, i=8),
-                in_=w4w_raw[:, 2 * PASS * b:2 * PASS * (b + 1)].bitcast(U16).rearrange("p (c i t) -> p c t i", t=PACK, i=8))
             nc.vector.tensor_copy(
                 out=scales[:].rearrange("p (t c i) -> p c t i", t=PACK, i=16),
                 in_=w4s_raw[:, PASS * b:PASS * (b + 1)].rearrange("p (c i t) -> p c t i", t=PACK, i=16))
-            w4w.append(words)
             w4s.append(scales)
 
-        def round_w1(raw, grouped, lo, hi):
-            nc.scalar.copy(out=grouped[:].rearrange("p (t m j) -> p m t j", t=PACK, j=PACK)[:, lo:hi],
+        def round_w1(raw, grouped, lo, hi, copy):
+            copy(out=grouped[:].rearrange("p (t m j) -> p m t j", t=PACK, j=PACK)[:, lo:hi],
                            in_=raw[:].rearrange("p j (m t) -> p m t j", t=PACK)[:, lo:hi])
 
         def quantise_w1(b, grouped):
@@ -109,18 +108,18 @@ def tile_list_mouth_piece_chooser_kernel(tc, tab_words, tab_scales, offs, tab2_w
 
         w1_bf0 = keep.tile([P, PACK * PASS], BF16, name="w1_bf0", align_bytes=64)
         w1_bf1 = keep.tile([P, PACK * PASS], BF16, name="w1_bf1", align_bytes=64)
-        round_w1(w1_raw0, w1_bf0, 0, P)
+        round_w1(w1_raw0, w1_bf0, 0, P, nc.scalar.copy)
         gather_v_scales(0)
-        gather_v_scales(1)
         deal_w4(0)
-        deal_w4(1)
         quantise_w1(0, w1_bf0)
+        gather_v_scales(1)
+        deal_w4(1)
         gather_v_words(0)
         gather_v_words(1)
 
         w1_raw1 = load_w1(1)
         tab2_s = keep.tile([P, T3], U8, name="tab2_s", tag="scale_rows", align_bytes=64)
-        nc.vector.memset(tab2_s[:].bitcast(I32), 0)
+        nc.gpsimd.memset(tab2_s[:].bitcast(I32), 0)
         for q in range(4):
             nc.sync.dma_start(tab2_s[32 * q:32 * q + 8, :].bitcast(I32), tab2_scales[:, 4 * q:4 * q + 4, :].bitcast(I32))
         v2s = keep.tile([P, S2], U8, name="v2s", align_bytes=64)
@@ -140,25 +139,46 @@ def tile_list_mouth_piece_chooser_kernel(tc, tab_words, tab_scales, offs, tab2_w
         groups = [(0, 0, 512), (0, 512, 512), (1, 0, 512), (1, 512, 256), (1, 768, 256)]
         bounded, hw, hs = {}, {}, {}
 
-        def unit(g, t):
+        units = [(g, t) for g in range(len(groups)) for t in range(PACK)]
+        stress_ps, shape_ps, stress, prod = {}, {}, {}, {}
+
+        def moving(g):
             b, c0, width = groups[g]
             h, lo = divmod(c0, HALF)
-            cols = slice(lo, lo + width)
+            return vw[h][:, lo:lo + width].bitcast(FP8X4), vs[h][:, lo:lo + width]
+
+        def stress_product(u):
+            b, h, t = u // 8, u // 4 % 2, u % 4
+            rhs, rhs_scale = vw[h][:].bitcast(FP8X4), vs[h][:]
+            stress_ps[u] = psum.tile([P, HALF], F32, name="stress_ps", tag="stress_ps", bufs=3)
+            nc.tensor.matmul_mx(out=stress_ps[u][:], lhsT=w4w[:, 2 * P * (PACK * b + t):2 * P * (PACK * b + t + 1)].bitcast(FP4X4),
+                                lhsT_scale=w4s[b][:, P * t:P * (t + 1)], rhs=rhs, rhs_scale=rhs_scale, start=True, stop=True)
+
+        def shape_product(u):
+            g, t = units[u]
+            b, c0, width = groups[g]
+            rhs, rhs_scale = moving(g)
+            shape_ps[u] = psum.tile([P, width], F32, name="shape_ps", tag="shape_ps", bufs=3)
+            nc.tensor.matmul_mx(out=shape_ps[u][:], lhsT=w1w[b][:, P * t:P * (t + 1)].bitcast(FP8X4),
+                                lhsT_scale=w1s[b][:, P * t:P * (t + 1)], rhs=rhs, rhs_scale=rhs_scale, start=True, stop=True)
+
+        def stress_out(u):
+            stress[u] = work.tile([P, HALF], F32, name="stress", tag="stress", bufs=8)
+            nc.scalar.copy(out=stress[u][:], in_=stress_ps[u][:])
+
+        def multiply(u):
+            g, t = units[u]
+            b, c0, width = groups[g]
+            h, lo = divmod(c0, HALF)
+            prod[u] = work.tile([P, width], F32, name="prod", tag="prod", bufs=3)
+            nc.vector.tensor_tensor(out=prod[u][:], in0=shape_ps[u][:], in1=stress[8 * b + 4 * h + t][:, lo:lo + width], op=ALU.mult)
+
+        def bound(u):
+            g, t = units[u]
+            b, c0, width = groups[g]
             if t == 0:
                 bounded[g] = work.tile([P, PACK, width], F32, name="bounded", tag="bounded")
-            stress_ps = psum.tile([P, width], F32, name="stress_ps", tag="stress_ps", bufs=3)
-            nc.tensor.matmul_mx(out=stress_ps[:], lhsT=w4w[b][:, 2 * P * t:2 * P * (t + 1)].bitcast(FP4X4),
-                                lhsT_scale=w4s[b][:, P * t:P * (t + 1)], rhs=vw[h][:, cols].bitcast(FP8X4),
-                                rhs_scale=vs[h][:, cols], start=True, stop=True)
-            shape_ps = psum.tile([P, width], F32, name="shape_ps", tag="shape_ps", bufs=3)
-            nc.tensor.matmul_mx(out=shape_ps[:], lhsT=w1w[b][:, P * t:P * (t + 1)].bitcast(FP8X4),
-                                lhsT_scale=w1s[b][:, P * t:P * (t + 1)], rhs=vw[h][:, cols].bitcast(FP8X4),
-                                rhs_scale=vs[h][:, cols], start=True, stop=True)
-            stress = work.tile([P, width], F32, name="stress", tag="stress", bufs=4)
-            nc.scalar.copy(out=stress[:], in_=stress_ps[:])
-            prod = work.tile([P, width], F32, name="prod", tag="prod", bufs=3)
-            nc.vector.tensor_tensor(out=prod[:], in0=shape_ps[:], in1=stress[:], op=ALU.mult)
-            nc.scalar.activation(out=bounded[g][:, t, :], in_=prod[:], func=ACT.Tanh, bias=rest_t[:, b, t:t + 1])
+            nc.scalar.activation(out=bounded[g][:, t, :], in_=prod[u][:], func=ACT.Tanh, bias=rest_t[:, b, t:t + 1])
 
         h_bf = {}
 
@@ -177,10 +197,10 @@ def tile_list_mouth_piece_chooser_kernel(tc, tab_words, tab_scales, offs, tab2_w
             hs[g] = keep.tile([P, width], U8, name=f"hs{g}", align_bytes=64)
             nc.vector.quantize_mx(out=hw[g][:].bitcast(FP8X4), scales=hs[g][:], in_=h_bf[g][:])
 
-        def scores(g):
+        def scores(g, ms):
             b, c0, width = groups[g]
             g0, lo = divmod(c0, HALF)
-            for m in range(4):
+            for m in ms:
                 e_ps = psum.tile([P, width], F32, name="e_ps", tag="e_ps", bufs=2)
                 for a, (gg, cols) in enumerate(((g0, slice(lo, lo + width)), (g, slice(0, width)))):
                     nc.tensor.matmul_mx(out=e_ps[:], lhsT=v2w[a][:, P * m:P * (m + 1)].bitcast(FP8X4),
@@ -189,30 +209,46 @@ def tile_list_mouth_piece_chooser_kernel(tc, tab_words, tab_scales, offs, tab2_w
                 nc.scalar.activation(out=neg_e[m][:, c0:c0 + width], in_=e_ps[:], func=ACT.Copy, scale=-1.0)
 
         shot_t = keep.tile([P, 4, NP], F32, name="shot_t", tag="stage")
-        for g in range(len(groups)):
-            for t in range(PACK):
-                unit(g, t)
-                u = PACK * g + t
-                if g > 0 and t == 1:
-                    apply_gain(g - 1)
-                if g > 0 and t == 2:
-                    quantise_h(g - 1)
-                if g > 2 and t == 3:
-                    scores(g - 1)
-                if 2 <= u < 6:
-                    round_w1(w1_raw1, w1_bf1, 32 * (u - 2), 32 * (u - 1))
-                if u == 5:
-                    nc.sync.dma_start(shot_t[:], shot.rearrange("(m p) n -> p m n", p=P))
-                if u == 6:
-                    quantise_w1(1, w1_bf1)
-                if u == 8:
-                    nc.vector.tensor_copy(v2s[:], tab2_s[:].indirect(offs2_t[:]))
-                if u in (10, 11):
-                    gather_v2_words(u - 10)
+        n_units = len(units)
+        for u in range(-3, n_units + 1):
+            if 0 <= u + 3 < 12:
+                stress_product(u + 3)
+            if 8 <= u < 12:
+                stress_product(u + 4)
+            if 0 <= u + 2 < n_units:
+                shape_product(u + 2)
+            if 0 <= u + 2 < 12:
+                stress_out(u + 2)
+            if 0 <= u < n_units:
+                multiply(u)
+            if 0 <= u - 1 < n_units:
+                bound(u - 1)
+            if 8 <= u < 12:
+                stress_out(u + 4)
+            g, t = divmod(u, PACK)
+            if 0 < g < len(groups) and t == 2:
+                apply_gain(g - 1)
+            if 0 < g < len(groups) and t == 3:
+                quantise_h(g - 1)
+            if 0 <= u < 4:
+                round_w1(w1_raw1, w1_bf1, 32 * u, 32 * (u + 1), nc.vector.tensor_copy if u < 3 else nc.scalar.copy)
+            if u == 3:
+                nc.vector.tensor_copy(v2s[:], tab2_s[:].indirect(offs2_t[:]))
+                nc.sync.dma_start(shot_t[:], shot.rearrange("(m p) n -> p m n", p=P))
+            if u == 4:
+                quantise_w1(1, w1_bf1)
+            if u in (7, 8):
+                gather_v2_words(u - 7)
+            if u >= n_units - 1:
+                scores(2, [u - n_units + 1])
         last = len(groups) - 1
         apply_gain(last)
+        scores(last - 1, (0, 1))
         quantise_h(last)
-        scores(last)
+        scores(last, (0, 1))
+        for m in (2, 3):
+            for g in range(2, last + 1):
+                scores(g, [m])
 
         scaled = {}
 
@@ -221,9 +257,13 @@ def tile_list_mouth_piece_chooser_kernel(tc, tab_words, tab_scales, offs, tab2_w
             nc.vector.tensor_tensor(scaled[m][:], neg_e[m][:].indirect(pos1_t[:]), shot_t[:, m, :], ALU.mult)
 
         def outgoing(m):
-            res = work.tile([P, NP], F32, name="res", tag="res", bufs=4)
-            nc.vector.tensor_tensor(res[:], neg_e[m][:].indirect(pos2_t[:]), scaled[m][:], ALU.subtract)
-            nc.sync.dma_start(out[P * m:P * (m + 1), :], res[:])
+            pieces = 2 if m == 3 else 1
+            n = NP // pieces
+            for i in range(pieces):
+                res = work.tile([P, n], F32, name="res", tag="res", bufs=5)
+                nc.vector.tensor_tensor(res[:], neg_e[m][:].indirect(pos2_t[:, i * n // 16:(i + 1) * n // 16]),
+                                        scaled[m][:, i * n:(i + 1) * n], ALU.subtract)
+                nc.sync.dma_start(out[P * m:P * (m + 1), i * n:(i + 1) * n], res[:])
 
         incoming(0)
         for m in range(4):

@@ -28,6 +28,7 @@ def tile_list_mouth_piece_chooser_kernel(tc, tab_words, tab_scales, offs, tab2_w
     with ExitStack() as ctx:
         keep = ctx.enter_context(tc.tile_pool(name="keep", bufs=1))
         work = ctx.enter_context(tc.tile_pool(name="work", bufs=2))
+        turns = ctx.enter_context(tc.tile_pool(name="turns", bufs=1))
         psum = ctx.enter_context(tc.psum_pool(name="psum", bufs=1))
 
         offs_t = keep.tile([P, S // 16], U16, name="offs_t")
@@ -37,21 +38,22 @@ def tile_list_mouth_piece_chooser_kernel(tc, tab_words, tab_scales, offs, tab2_w
 
         w4s_raw = keep.tile([P, H], U8, name="w4s_raw", tag="scale_rows", align_bytes=64)
         tab_s = keep.tile([P, T], U8, name="tab_s", align_bytes=64)
-        warm = keep.tile([P, 2], F32, name="warm", tag="rows")
         nc.gpsimd.memset(w4s_raw[:].bitcast(I32), 0)
         nc.vector.memset(tab_s[:].bitcast(I32), 0)
-        nc.vector.memset(warm[:, 0:1], 0.0)
 
         w1_rows = w1.rearrange("(p j) c -> p j c", j=PACK)
 
         def load_w1(b):
-            raw = keep.tile([P, PACK, PASS], F32, name="w1_raw", tag="stage")
+            if b == 0:
+                raw = keep.tile([P, PACK, PASS], F32, name="w1_raw0", tag="stage")
+            else:
+                raw = turns.tile([P, PACK, PASS], F32, name="w1_raw1", align_bytes=64, offset=4 * T + 64)
             nc.sync.dma_start(raw[:], w1_rows[:, :, b * PASS:(b + 1) * PASS])
             return raw
 
-        w4w_raw = keep.tile([P, 2 * H], U8, name="w4w_raw", tag="table", align_bytes=64)
-        nc.sync.dma_start(w4w_raw[:].bitcast(I32), w4_words[0].bitcast(I32))
         nc.sync.dma_start(offs_t[:], offs)
+        w4w_raw = turns.tile([P, 2 * H], U8, name="w4w_raw", align_bytes=64, offset=4 * T - H)
+        nc.sync.dma_start(w4w_raw[:].bitcast(I32), w4_words[0].bitcast(I32))
         nc.sync.dma_start(offs2_t[:], offs2)
         for q in range(4):
             nc.scalar.dma_start(tab_s[32 * q:32 * q + 4, :].bitcast(I32), tab_scales[0, 4 * q:4 * q + 4, :].bitcast(I32))
@@ -62,14 +64,13 @@ def tile_list_mouth_piece_chooser_kernel(tc, tab_words, tab_scales, offs, tab2_w
         nc.vector.tensor_copy(
             out=w4w[:].bitcast(U16).rearrange("p (b t c i) -> p b c t i", b=2, t=PACK, i=8),
             in_=w4w_raw[:].bitcast(U16).rearrange("p (b c i t) -> p b c t i", b=2, t=PACK, i=8))
-        tab_w = keep.tile([P, T], I32, name="tab_w", tag="table", align_bytes=64)
+        tab_w = turns.tile([P, T], I32, name="tab_w", align_bytes=64, offset=0)
         nc.sync.dma_start(tab_w[:], tab_words[0].rearrange("p n t -> p (n t)").bitcast(I32))
 
         for q in range(4):
-            queue = nc.scalar if q < 3 else nc.gpsimd
+            queue = nc.scalar if q < 2 else nc.gpsimd
             queue.dma_start(w4s_raw[32 * q:32 * q + 4, :].bitcast(I32), w4_scales[0, 4 * q:4 * q + 4, :].bitcast(I32))
-        nc.scalar.activation(out=warm[:, 1:2], in_=warm[:, 0:1], func=ACT.Tanh)
-        rows = keep.tile([P, 2, 2, PACK], F32, name="rows", tag="rows")
+        rows = turns.tile([P, 2, 2, PACK], F32, name="rows", align_bytes=64, offset=4 * T)
         rest_t, gain_t = rows[:, 0], rows[:, 1]
         nc.gpsimd.dma_start(rest_t, rest.rearrange("(b p t) -> p b t", b=2, t=PACK))
         nc.gpsimd.dma_start(gain_t, gain.rearrange("(b p t) -> p b t", b=2, t=PACK))
@@ -82,6 +83,9 @@ def tile_list_mouth_piece_chooser_kernel(tc, tab_words, tab_scales, offs, tab2_w
                 out=scales[:].rearrange("p (t c i) -> p c t i", t=PACK, i=16),
                 in_=w4s_raw[:, PASS * b:PASS * (b + 1)].rearrange("p (c i t) -> p c t i", t=PACK, i=16))
             w4s.append(scales)
+
+        def gpsimd_round(out, in_):
+            nc.gpsimd.tensor_scalar(out=out, in0=in_, scalar1=1.0, scalar2=0.0, op0=ALU.mult, op1=ALU.add)
 
         def round_w1(raw, grouped, lo, hi, copy):
             copy(out=grouped[:].rearrange("p (t m j) -> p m t j", t=PACK, j=PACK)[:, lo:hi],
@@ -110,9 +114,9 @@ def tile_list_mouth_piece_chooser_kernel(tc, tab_words, tab_scales, offs, tab2_w
         w1_bf1 = keep.tile([P, PACK * PASS], BF16, name="w1_bf1", align_bytes=64)
         round_w1(w1_raw0, w1_bf0, 0, P, nc.scalar.copy)
         gather_v_scales(0)
+        gather_v_scales(1)
         deal_w4(0)
         quantise_w1(0, w1_bf0)
-        gather_v_scales(1)
         deal_w4(1)
         gather_v_words(0)
         gather_v_words(1)
@@ -123,7 +127,7 @@ def tile_list_mouth_piece_chooser_kernel(tc, tab_words, tab_scales, offs, tab2_w
         for q in range(4):
             nc.sync.dma_start(tab2_s[32 * q:32 * q + 8, :].bitcast(I32), tab2_scales[:, 4 * q:4 * q + 4, :].bitcast(I32))
         v2s = keep.tile([P, S2], U8, name="v2s", align_bytes=64)
-        tab2_w = keep.tile([P, 2 * T3], I32, name="tab2_w", tag="table", align_bytes=64)
+        tab2_w = turns.tile([P, 2 * T3], I32, name="tab2_w", align_bytes=64, offset=0)
         for a in range(2):
             nc.sync.dma_start(tab2_w[:, a * T3:(a + 1) * T3], tab2_words[a].rearrange("p n t -> p (n t)").bitcast(I32))
 
@@ -177,19 +181,22 @@ def tile_list_mouth_piece_chooser_kernel(tc, tab_words, tab_scales, offs, tab2_w
             g, t = units[u]
             b, c0, width = groups[g]
             if t == 0:
-                bounded[g] = work.tile([P, PACK, width], F32, name="bounded", tag="bounded")
+                bounded[g] = work.tile([P, PACK, width], F32, name="bounded", tag="bounded", bufs=3)
             nc.scalar.activation(out=bounded[g][:, t, :], in_=prod[u][:], func=ACT.Tanh, bias=rest_t[:, b, t:t + 1])
 
         h_bf = {}
 
         def apply_gain(g):
             b, c0, width = groups[g]
-            h_bf[g] = work.tile([P, PACK * width], BF16, name="h_bf", tag="h_bf", align_bytes=64)
-            nc.vector.tensor_tensor(
-                out=h_bf[g][:].rearrange("p (c i t) -> p c t i", t=PACK, i=4),
-                in0=bounded[g][:].rearrange("p t (c i) -> p c t i", i=4),
-                in1=gain_t[:, b, :].unsqueeze(1).unsqueeze(3).to_broadcast([P, width // 4, PACK, 4]),
-                op=ALU.mult)
+            h_bf[g] = work.tile([P, PACK * width], BF16, name="h_bf", tag="h_bf", bufs=3, align_bytes=64)
+            engine, pieces = nc.vector, 1
+            n = width // 4 // pieces
+            for i in range(pieces):
+                engine.tensor_tensor(
+                    out=h_bf[g][:].rearrange("p (c i t) -> p c t i", t=PACK, i=4)[:, i * n:(i + 1) * n],
+                    in0=bounded[g][:].rearrange("p t (c i) -> p c t i", i=4)[:, i * n:(i + 1) * n],
+                    in1=gain_t[:, b, :].unsqueeze(1).unsqueeze(3).to_broadcast([P, n, PACK, 4]),
+                    op=ALU.mult)
 
         def quantise_h(g):
             b, c0, width = groups[g]
@@ -223,15 +230,15 @@ def tile_list_mouth_piece_chooser_kernel(tc, tab_words, tab_scales, offs, tab2_w
                 multiply(u)
             if 0 <= u - 1 < n_units:
                 bound(u - 1)
-            if 8 <= u < 12:
-                stress_out(u + 4)
+            if 9 <= u < 13:
+                stress_out(u + 3)
             g, t = divmod(u, PACK)
             if 0 < g < len(groups) and t == 2:
                 apply_gain(g - 1)
             if 0 < g < len(groups) and t == 3:
                 quantise_h(g - 1)
-            if 0 <= u < 4:
-                round_w1(w1_raw1, w1_bf1, 32 * u, 32 * (u + 1), nc.vector.tensor_copy if u < 3 else nc.scalar.copy)
+            if -1 <= u < 3:
+                round_w1(w1_raw1, w1_bf1, 32 * (u + 1), 32 * (u + 2), gpsimd_round)
             if u == 3:
                 nc.vector.tensor_copy(v2s[:], tab2_s[:].indirect(offs2_t[:]))
                 nc.sync.dma_start(shot_t[:], shot.rearrange("(m p) n -> p m n", p=P))

from contextlib import ExitStack

import concourse.mybir as mybir

K, H, T, S, S2, T3, NP = 512, 1024, 4096, 1024, 512, 2048, 512
FLOPS = 2 * K * H * S * 2 + 2 * H * S2 * S

F32 = mybir.dt.float32
BF16 = mybir.dt.bfloat16
I32 = mybir.dt.int32
U32 = mybir.dt.uint32
U16 = mybir.dt.uint16
U8 = mybir.dt.uint8
FP8X4 = mybir.dt.float8_e4m3fn_x4
FP4X4 = mybir.dt.float4_e2m1fn_x4
ACT = mybir.ActivationFunctionType
ALU = mybir.AluOpType

P = 128
PACK = 4
PASS = P * PACK
HALF = 512


def tile_list_mouth_piece_chooser_kernel(tc, tab_words, tab_scales, offs, tab2_words, tab2_scales, offs2,
                                                  pos1, pos2, w1, w4_words, w4_scales, rest, gain, shot, out):
    nc = tc.nc
    with ExitStack() as ctx:
        keep = ctx.enter_context(tc.tile_pool(name="keep", bufs=1))
        work = ctx.enter_context(tc.tile_pool(name="work", bufs=2))
        turns = ctx.enter_context(tc.tile_pool(name="turns", bufs=1))
        psum = ctx.enter_context(tc.psum_pool(name="psum", bufs=1))

        offs_t = keep.tile([P, S // 16], U16, name="offs_t")
        offs2_t = keep.tile([P, S2 // 16], U16, name="offs2_t")
        pos1_t = keep.tile([P, NP // 16], U16, name="pos1_t")
        pos2_t = keep.tile([P, NP // 16], U16, name="pos2_t")

        w4s_raw = keep.tile([P, H], U8, name="w4s_raw", tag="scale_rows", align_bytes=64)
        tab_s = keep.tile([P, T], U8, name="tab_s", align_bytes=64)
        nc.gpsimd.memset(w4s_raw[:].bitcast(I32), 0)
        nc.vector.memset(tab_s[:].bitcast(I32), 0)

        w1_rows = w1.rearrange("(p j) c -> p j c", j=PACK)

        def load_w1(b):
            if b == 0:
                raw = keep.tile([P, PACK, PASS], F32, name="w1_raw0", tag="stage")
            else:
                raw = turns.tile([P, PACK, PASS], F32, name="w1_raw1", align_bytes=64, offset=4 * T + 64)
            nc.sync.dma_start(raw[:], w1_rows[:, :, b * PASS:(b + 1) * PASS])
            return raw

        nc.sync.dma_start(offs_t[:], offs)
        w4w_raw = turns.tile([P, 2 * H], U8, name="w4w_raw", align_bytes=64, offset=4 * T - H)
        nc.sync.dma_start(w4w_raw[:].bitcast(I32), w4_words[0].bitcast(I32))
        nc.sync.dma_start(offs2_t[:], offs2)
        for q in range(4):
            nc.scalar.dma_start(tab_s[32 * q:32 * q + 4, :].bitcast(I32), tab_scales[0, 4 * q:4 * q + 4, :].bitcast(I32))
        nc.sync.dma_start(pos1_t[:], pos1)
        nc.sync.dma_start(pos2_t[:], pos2)
        w1_raw0 = load_w1(0)
        w4w = keep.tile([P, 2 * H], U8, name="w4w", align_bytes=64)
        nc.vector.tensor_copy(
            out=w4w[:].bitcast(U16).rearrange("p (b t c i) -> p b c t i", b=2, t=PACK, i=8),
            in_=w4w_raw[:].bitcast(U16).rearrange("p (b c i t) -> p b c t i", b=2, t=PACK, i=8))
        tab_w = turns.tile([P, T], I32, name="tab_w", align_bytes=64, offset=0)
        nc.sync.dma_start(tab_w[:], tab_words[0].rearrange("p n t -> p (n t)").bitcast(I32))

        for q in range(4):
            queue = nc.scalar if q < 2 else nc.gpsimd
            queue.dma_start(w4s_raw[32 * q:32 * q + 4, :].bitcast(I32), w4_scales[0, 4 * q:4 * q + 4, :].bitcast(I32))
        rows = turns.tile([P, 2, 2, PACK], F32, name="rows", align_bytes=64, offset=4 * T)
        rest_t, gain_t = rows[:, 0], rows[:, 1]
        nc.gpsimd.dma_start(rest_t, rest.rearrange("(b p t) -> p b t", b=2, t=PACK))
        nc.gpsimd.dma_start(gain_t, gain.rearrange("(b p t) -> p b t", b=2, t=PACK))

        w4s, w1w, w1s = [], [], []

        def deal_w4(b):
            scales = keep.tile([P, PASS], U8, name=f"w4s{b}", align_bytes=64)
            nc.vector.tensor_copy(
                out=scales[:].rearrange("p (t c i) -> p c t i", t=PACK, i=16),
                in_=w4s_raw[:, PASS * b:PASS * (b + 1)].rearrange("p (c i t) -> p c t i", t=PACK, i=16))
            w4s.append(scales)

        def gpsimd_round(out, in_):
            nc.gpsimd.tensor_scalar(out=out, in0=in_, scalar1=1.0, scalar2=0.0, op0=ALU.mult, op1=ALU.add)

        def round_w1(raw, grouped, lo, hi, copy):
            copy(out=grouped[:].rearrange("p (t m j) -> p m t j", t=PACK, j=PACK)[:, lo:hi],
                           in_=raw[:].rearrange("p j (m t) -> p m t j", t=PACK)[:, lo:hi])

        def quantise_w1(b, grouped):
            words = keep.tile([P, PASS], U32, name=f"w1w{b}", align_bytes=64)
            scales = keep.tile([P, PASS], U8, name=f"w1s{b}", align_bytes=64)
            nc.vector.quantize_mx(out=words[:].bitcast(FP8X4), scales=scales[:], in_=grouped[:])
            w1w.append(words)
            w1s.append(scales)

        vs, vw = [], []

        def gather_v_scales(h):
            t = keep.tile([P, HALF], U8, name=f"vs{h}", align_bytes=64)
            nc.vector.tensor_copy(t[:], tab_s[:].indirect(offs_t[:, 32 * h:32 * (h + 1)]))
            vs.append(t)

        def gather_v_words(h):
            t = keep.tile([P, HALF], U32, name=f"vw{h}", align_bytes=64)
            nc.vector.tensor_copy(t[:], tab_w[:].bitcast(U32).indirect(offs_t[:, 32 * h:32 * (h + 1)]))
            vw.append(t)

        w1_bf0 = keep.tile([P, PACK * PASS], BF16, name="w1_bf0", align_bytes=64)
        w1_bf1 = keep.tile([P, PACK * PASS], BF16, name="w1_bf1", align_bytes=64)
        round_w1(w1_raw0, w1_bf0, 0, P, nc.scalar.copy)
        gather_v_scales(0)
        gather_v_scales(1)
        deal_w4(0)
        quantise_w1(0, w1_bf0)
        deal_w4(1)
        gather_v_words(0)
        gather_v_words(1)

        w1_raw1 = load_w1(1)
        tab2_s = keep.tile([P, T3], U8, name="tab2_s", tag="scale_rows", align_bytes=64)
        nc.gpsimd.memset(tab2_s[:].bitcast(I32), 0)
        for q in range(4):
            nc.sync.dma_start(tab2_s[32 * q:32 * q + 8, :].bitcast(I32), tab2_scales[:, 4 * q:4 * q + 4, :].bitcast(I32))
        v2s = keep.tile([P, S2], U8, name="v2s", align_bytes=64)
        tab2_w = turns.tile([P, 2 * T3], I32, name="tab2_w", align_bytes=64, offset=0)
        for a in range(2):
            nc.sync.dma_start(tab2_w[:, a * T3:(a + 1) * T3], tab2_words[a].rearrange("p n t -> p (n t)").bitcast(I32))

        v2w = []

        def gather_v2_words(a):
            t = keep.tile([P, S2], U32, name=f"v2w{a}", align_bytes=64)
            nc.vector.tensor_copy(t[:], tab2_w[:, a * T3:(a + 1) * T3].bitcast(U32).indirect(offs2_t[:]))
            v2w.append(t)

        neg_e = [keep.tile([P, S], F32, name=f"neg_e{m}") for m in range(4)]

        groups = [(0, 0, 512), (0, 512, 512), (1, 0, 512), (1, 512, 256), (1, 768, 256)]
        bounded, hw, hs = {}, {}, {}

        units = [(g, t) for g in range(len(groups)) for t in range(PACK)]
        stress_ps, shape_ps, stress, prod = {}, {}, {}, {}

        def moving(g):
            b, c0, width = groups[g]
            h, lo = divmod(c0, HALF)
            return vw[h][:, lo:lo + width].bitcast(FP8X4), vs[h][:, lo:lo + width]

        def stress_product(u):
            b, h, t = u // 8, u // 4 % 2, u % 4
            rhs, rhs_scale = vw[h][:].bitcast(FP8X4), vs[h][:]
            stress_ps[u] = psum.tile([P, HALF], F32, name="stress_ps", tag="stress_ps", bufs=3)
            nc.tensor.matmul_mx(out=stress_ps[u][:], lhsT=w4w[:, 2 * P * (PACK * b + t):2 * P * (PACK * b + t + 1)].bitcast(FP4X4),
                                lhsT_scale=w4s[b][:, P * t:P * (t + 1)], rhs=rhs, rhs_scale=rhs_scale, start=True, stop=True)

        def shape_product(u):
            g, t = units[u]
            b, c0, width = groups[g]
            rhs, rhs_scale = moving(g)
            shape_ps[u] = psum.tile([P, width], F32, name="shape_ps", tag="shape_ps", bufs=3)
            nc.tensor.matmul_mx(out=shape_ps[u][:], lhsT=w1w[b][:, P * t:P * (t + 1)].bitcast(FP8X4),
                                lhsT_scale=w1s[b][:, P * t:P * (t + 1)], rhs=rhs, rhs_scale=rhs_scale, start=True, stop=True)

        def stress_out(u):
            stress[u] = work.tile([P, HALF], F32, name="stress", tag="stress", bufs=8)
            nc.scalar.copy(out=stress[u][:], in_=stress_ps[u][:])

        def multiply(u):
            g, t = units[u]
            b, c0, width = groups[g]
            h, lo = divmod(c0, HALF)
            prod[u] = work.tile([P, width], F32, name="prod", tag="prod", bufs=3)
            nc.vector.tensor_tensor(out=prod[u][:], in0=shape_ps[u][:], in1=stress[8 * b + 4 * h + t][:, lo:lo + width], op=ALU.mult)

        def bound(u):
            g, t = units[u]
            b, c0, width = groups[g]
            if t == 0:
                bounded[g] = work.tile([P, PACK, width], F32, name="bounded", tag="bounded", bufs=3)
            nc.scalar.activation(out=bounded[g][:, t, :], in_=prod[u][:], func=ACT.Tanh, bias=rest_t[:, b, t:t + 1])

        h_bf = {}

        def apply_gain(g):
            b, c0, width = groups[g]
            h_bf[g] = work.tile([P, PACK * width], BF16, name="h_bf", tag="h_bf", bufs=3, align_bytes=64)
            engine, pieces = nc.vector, 1
            n = width // 4 // pieces
            for i in range(pieces):
                engine.tensor_tensor(
                    out=h_bf[g][:].rearrange("p (c i t) -> p c t i", t=PACK, i=4)[:, i * n:(i + 1) * n],
                    in0=bounded[g][:].rearrange("p t (c i) -> p c t i", i=4)[:, i * n:(i + 1) * n],
                    in1=gain_t[:, b, :].unsqueeze(1).unsqueeze(3).to_broadcast([P, n, PACK, 4]),
                    op=ALU.mult)

        def quantise_h(g):
            b, c0, width = groups[g]
            hw[g] = keep.tile([P, width], U32, name=f"hw{g}", align_bytes=64)
            hs[g] = keep.tile([P, width], U8, name=f"hs{g}", align_bytes=64)
            nc.vector.quantize_mx(out=hw[g][:].bitcast(FP8X4), scales=hs[g][:], in_=h_bf[g][:])

        def scores(g, ms):
            b, c0, width = groups[g]
            g0, lo = divmod(c0, HALF)
            for m in ms:
                e_ps = psum.tile([P, width], F32, name="e_ps", tag="e_ps", bufs=2)
                for a, (gg, cols) in enumerate(((g0, slice(lo, lo + width)), (g, slice(0, width)))):
                    nc.tensor.matmul_mx(out=e_ps[:], lhsT=v2w[a][:, P * m:P * (m + 1)].bitcast(FP8X4),
                                        lhsT_scale=v2s[4 * a:P, P * m:P * (m + 1)], rhs=hw[gg][:, cols].bitcast(FP8X4),
                                        rhs_scale=hs[gg][:, cols], start=(a == 0), stop=(a == 1))
                nc.scalar.activation(out=neg_e[m][:, c0:c0 + width], in_=e_ps[:], func=ACT.Copy, scale=-1.0)

        shot_t = keep.tile([P, 4, NP], F32, name="shot_t", tag="stage")
        n_units = len(units)
        for u in range(-3, n_units + 1):
            if 0 <= u + 3 < 12:
                stress_product(u + 3)
            if 8 <= u < 12:
                stress_product(u + 4)
            if 0 <= u + 2 < n_units:
                shape_product(u + 2)
            if 0 <= u + 2 < 12:
                stress_out(u + 2)
            if 0 <= u < n_units:
                multiply(u)
            if 0 <= u - 1 < n_units:
                bound(u - 1)
            if 9 <= u < 13:
                stress_out(u + 3)
            g, t = divmod(u, PACK)
            if 0 < g < len(groups) and t == 2:
                apply_gain(g - 1)
            if 0 < g < len(groups) and t == 3:
                quantise_h(g - 1)
            if -1 <= u < 3:
                round_w1(w1_raw1, w1_bf1, 32 * (u + 1), 32 * (u + 2), gpsimd_round)
            if u == 3:
                nc.vector.tensor_copy(v2s[:], tab2_s[:].indirect(offs2_t[:]))
                nc.sync.dma_start(shot_t[:], shot.rearrange("(m p) n -> p m n", p=P))
            if u == 4:
                quantise_w1(1, w1_bf1)
            if u in (7, 8):
                gather_v2_words(u - 7)
            if u >= n_units - 1:
                scores(2, [u - n_units + 1])
        last = len(groups) - 1
        apply_gain(last)
        scores(last - 1, (0, 1))
        quantise_h(last)
        scores(last, (0, 1))
        for m in (2, 3):
            for g in range(2, last + 1):
                scores(g, [m])

        scaled = {}

        def incoming(m):
            scaled[m] = work.tile([P, NP], F32, name="scaled", tag="scaled")
            nc.vector.tensor_tensor(scaled[m][:], neg_e[m][:].indirect(pos1_t[:]), shot_t[:, m, :], ALU.mult)

        def outgoing(m):
            pieces = 2 if m == 3 else 1
            n = NP // pieces
            for i in range(pieces):
                res = work.tile([P, n], F32, name="res", tag="res", bufs=5)
                nc.vector.tensor_tensor(res[:], neg_e[m][:].indirect(pos2_t[:, i * n // 16:(i + 1) * n // 16]),
                                        scaled[m][:, i * n:(i + 1) * n], ALU.subtract)
                nc.sync.dma_start(out[P * m:P * (m + 1), i * n:(i + 1) * n], res[:])

        incoming(0)
        for m in range(4):
            if m < 3:
                incoming(m + 1)
            outgoing(m)
